import numpy as np
import ml_dtypes


def mxq(x, axis, fmt="e4m3"):
    dtype, down = {"e4m3": (ml_dtypes.float8_e4m3fn, 7), "e5m2": (ml_dtypes.float8_e5m2, 14)}[fmt]
    v = np.moveaxis(np.asarray(x, np.float32).astype(ml_dtypes.bfloat16).astype(np.float64), axis, -1)
    blocks = v.reshape(v.shape[:-1] + (-1, 32))
    amax = np.abs(blocks).max(-1, keepdims=True)
    byte = np.maximum(np.where(amax > 0, np.frexp(amax)[1] - 1 + 127, 0) - down, 1)
    scale = np.exp2(byte - 127.0)
    codes = (blocks / scale).astype(np.float32).astype(dtype).astype(np.float64)
    return np.moveaxis((codes * scale).reshape(v.shape), -1, axis)


WIDE = False


def mx_kscale(k):
    if not WIDE:
        return np.ones(k)
    levels = np.array([10, -10, 5, -5, 0])
    if k % 512:
        return np.exp2(np.random.permutation(np.resize(levels, k // 32))).repeat(32)
    a = np.empty((k // 512, 16))
    for p in range(k // 512):
        a[p, :8] = np.random.permutation(np.resize(levels, 8))
        for g in range(8):
            far = levels[np.abs(levels - a[p, g]) >= 10]
            a[p, g + 8] = far[np.random.randint(len(far))]
    return np.exp2(a.ravel()).repeat(32)


def f64(x):
    return np.asarray(x).astype(np.float64)


def striped(idx):
    return np.tile(np.asarray(idx).reshape(-1, 16).T, (8, 1)).astype(np.uint16)


def unstriped(offs):
    return offs[:16].T.reshape(-1).astype(np.int64)


E2M1 = np.array([0.0, 0.5, 1.0, 1.5, 2.0, 3.0, 4.0, 6.0, -0.0, -0.5, -1.0, -1.5, -2.0, -3.0, -4.0, -6.0])


def pack_weight(w, fmt):
    k, n = w.shape
    w = f64(np.asarray(w, np.float32).astype(ml_dtypes.bfloat16)).reshape(k // 32, 32, n)
    amax = np.abs(w).max(1)
    if fmt == "e4m3":
        byte = np.frexp(amax)[1] - 1 + 127 - 7
    else:
        mant, ex = np.frexp(amax / 6.0)
        byte = np.where(mant > 0.5, ex, ex - 1) + 127
    byte = np.clip(np.where(amax > 0, byte, 1), 1, 254)
    scaled = (w * np.exp2(127.0 - byte)[:, None, :]).reshape(k, n).astype(np.float32)
    by_word = np.ascontiguousarray(scaled.reshape(k // 512, 128, 4, n).transpose(0, 1, 3, 2))
    if fmt == "e4m3":
        words = by_word.astype(ml_dtypes.float8_e4m3fn).view(np.uint8)
    else:
        c = by_word.astype(ml_dtypes.float4_e2m1fn).view(np.uint8) & 0xF
        words = (c[..., 0::2] | (c[..., 1::2] << 4)).reshape(k // 512, 128, 2 * n)
    return np.ascontiguousarray(words), np.ascontiguousarray(byte.astype(np.uint8).reshape(k // 512, 16, n))


def unpack_weight(words, scales, fmt):
    g, _, n = scales.shape
    words = np.ascontiguousarray(words).reshape(g, 128, n, -1)
    if fmt == "e4m3":
        vals = words.view(ml_dtypes.float8_e4m3fn).astype(np.float64)
    else:
        nib = np.empty((g, 128, n, 4), np.uint8)
        nib[..., 0::2] = words & 0xF
        nib[..., 1::2] = words >> 4
        vals = E2M1[nib]
    vals = vals * np.repeat(np.exp2(scales.astype(np.float64) - 127.0), 8, axis=1)[..., None]
    return vals.transpose(0, 1, 3, 2).reshape(g * 512, n)


K, T, J, I, S, R, N = 1024, 2048, 1024, 512, 512, 512, 512


def setup_inputs():
    n = np.random.standard_normal
    idx = np.random.permutation(T)[:J]
    idx2 = np.random.permutation(J)[:I]
    idx3 = np.random.permutation(J)[:S]
    fk = mx_kscale(K)
    fr = mx_kscale(R)
    xqp = pack_weight(n((K, T)) / fk[:, None], "e4m3")
    wap = pack_weight(n((K, R)) * 1 / np.sqrt(K) * fk[:, None] * fr, "e2m1")
    dap = pack_weight(n((R, N)) * 1 / np.sqrt(R) / fr[:, None], "e4m3")
    dbp = pack_weight(n((R, N)) * 1 / np.sqrt(R) / fr[:, None], "e2m1")
    return {
        "xq_words": xqp[0],
        "xq_scales": xqp[1],
        "wa_words": wap[0],
        "wa_scales": wap[1],
        "da_words": dap[0],
        "da_scales": dap[1],
        "db_words": dbp[0],
        "db_scales": dbp[1],
        "offs": striped(idx),
        "offs2": striped(idx2),
        "offs3": striped(idx3),
    }


def reference(xq_words, xq_scales, wa_words, wa_scales, da_words, da_scales, db_words, db_scales, offs, offs2, offs3):
    idx = unstriped(offs)
    idx2 = unstriped(offs2)
    idx3 = unstriped(offs3)
    xqu = unpack_weight(xq_words, xq_scales, "e4m3")
    wau = unpack_weight(wa_words, wa_scales, "e2m1")
    dau = unpack_weight(da_words, da_scales, "e4m3")
    dbu = unpack_weight(db_words, db_scales, "e2m1")
    xqidxg = xqu[:, idx]
    a = wau.T @ xqidxg
    hid = np.maximum(a, 0.0)
    hididx2q = mxq(hid[:, idx2], 0, "e4m3")
    p = dau.T @ hididx2q
    hididx3q = mxq(hid[:, idx3], 0, "e4m3")
    q = dbu.T @ hididx3q
    pg = np.zeros((N, J))
    pg[:, idx2] = p
    qg = np.zeros((N, J))
    qg[:, idx3] = q
    y = pg + qg
    return y

@@ -1,0 +1,264 @@
+from contextlib import ExitStack
+
+import concourse.mybir as mybir
+from concourse.masks import make_identity
+
+K, T, J, I, S, R, N = 1024, 2048, 1024, 512, 512, 512, 512
+FLOPS = 2 * (K * R * J + R * N * I + R * N * S)
+
+F32 = mybir.dt.float32
+BF16 = mybir.dt.bfloat16
+I32 = mybir.dt.int32
+U32 = mybir.dt.uint32
+U16 = mybir.dt.uint16
+U8 = mybir.dt.uint8
+FP8X4 = mybir.dt.float8_e4m3fn_x4
+FP4X4 = mybir.dt.float4_e2m1fn_x4
+RELU = mybir.ActivationFunctionType.Relu
+ADD = mybir.AluOpType.add
+
+P = 128
+PACK = 4
+PASSES = K // (P * PACK)
+BANK = 512
+HALVES = J // BANK
+TILES = N // P
+QUADS = 4
+LIST_ROWS = 16
+
+
+def tile_list_expert_down_two_roads_kernel(
+    tc, xq_words, xq_scales, wa_words, wa_scales, da_words, da_scales, db_words, db_scales, offs, offs2, offs3, out
+):
+    nc = tc.nc
+    with ExitStack() as ctx:
+        lists = ctx.enter_context(tc.tile_pool(name="lists", bufs=1))
+        sb = ctx.enter_context(tc.tile_pool(name="sb", bufs=1))
+        late = ctx.enter_context(tc.tile_pool(name="late", bufs=1))
+        psum = ctx.enter_context(tc.psum_pool(name="psum", bufs=1))
+
+        def sbuf(name, shape, dtype, tag=None):
+            return sb.tile(shape, dtype, name=name, tag=tag or name, align_bytes=64)
+
+        def reused(name, shape, dtype, offset):
+            return late.tile(shape, dtype, name=name, offset=offset, align_bytes=64)
+
+        def bank(name, number):
+            return psum.tile([P, BANK], F32, name=name, tag="bank%d" % number)
+
+        tok_list = lists.tile([P, J // LIST_ROWS], U16, name="tok_list")
+        way_lists = [lists.tile([P, I // LIST_ROWS], U16, name="way_list%d" % w) for w in range(2)]
+
+        xs_table = sbuf("xs_table", [P, T], U8)
+        was_raw = reused("was_raw", [P, PASSES, R], U8, 13824)
+        xs_moved = sbuf("xs_moved", [P, J], U8)
+        nc.vector.memset(xs_table[:, 0 : T // 2].bitcast(I32), 0)
+        nc.gpsimd.memset(xs_table[:, T // 2 : T].bitcast(I32), 0)
+        nc.vector.memset(was_raw[:].rearrange("p z n -> p (z n)").bitcast(I32), 0)
+        nc.vector.memset(xs_moved[:].bitcast(I32), 0)
+        pages = {}
+        for b in range(2):
+            pages[0, b] = sbuf("page0_%d" % b, [P, J], F32)
+            nc.vector.memset(pages[0, b][:], 0.0)
+
+        wa_raw = reused("wa_raw", [P, PASSES, 2 * R], U8, 8192)
+        nc.sync.dma_start(tok_list[:], offs)
+        nc.scalar.dma_start(wa_raw[:].bitcast(I32), wa_words.rearrange("z p b -> p z b").bitcast(I32))
+        for q in range(QUADS):
+            queue = nc.sync if q < QUADS // 2 else nc.scalar
+            queue.dma_start(
+                xs_table[32 * q : 32 * q + 8, :].bitcast(I32), xq_scales[:, 4 * q : 4 * q + 4, :].bitcast(I32)
+            )
+        xw_table = [sbuf("xw_table0", [P, T], I32), reused("xw_table1", [P, T], I32, 0)]
+        for z in range(PASSES):
+            nc.sync.dma_start(xw_table[z][:], xq_words[z].rearrange("p n t -> p (n t)").bitcast(I32))
+        for q in range(QUADS):
+            queue = nc.scalar if q < QUADS // 2 else nc.gpsimd
+            queue.dma_start(
+                was_raw[32 * q : 32 * q + 4, :, :].bitcast(I32),
+                wa_scales[:, 4 * q : 4 * q + 4, :].rearrange("z r n -> r z n").bitcast(I32),
+            )
+        nc.sync.dma_start(way_lists[0][:], offs2)
+        nc.sync.dma_start(way_lists[1][:], offs3)
+
+        wa_dealt = [sbuf("wa_dealt0", [P, PASSES, 2, 2 * P], U8), reused("wa_dealt1", [P, PASSES, 2, 2 * P], U8, 0)]
+        was_dealt = [sbuf("was_dealt0", [P, PASSES, 2, P], U8), reused("was_dealt1", [P, PASSES, 2, P], U8, 1024)]
+
+        def deal_words(g):
+            by_slot = wa_raw[:].bitcast(U16).rearrange("p z (m t) -> p z t m", t=PACK)
+            nc.vector.tensor_copy(wa_dealt[g][:].bitcast(U16), by_slot[:, :, 2 * g : 2 * g + 2, :])
+
+        def deal_scales(g):
+            by_slot = was_raw[:].rearrange("p z (m t) -> p z t m", t=PACK)
+            nc.vector.tensor_copy(was_dealt[g][:], by_slot[:, :, 2 * g : 2 * g + 2, :])
+
+        xw = {}
+
+        def gather_words(z, h):
+            xw[z, h] = sbuf("xw%d_%d" % (z, h), [P, BANK], U32)
+            cols = BANK // LIST_ROWS
+            nc.vector.tensor_copy(
+                xw[z, h][:], xw_table[z][:].bitcast(U32).indirect(tok_list[:, h * cols : (h + 1) * cols])
+            )
+
+        deal_words(0)
+        xs_picked = sbuf("xs_picked", [P, J], U8)
+        nc.vector.tensor_copy(xs_picked[:], xs_table[:].indirect(tok_list[:]))
+        for q in range(QUADS):
+            nc.scalar.dma_start(
+                xs_moved[32 * q : 32 * q + 4, :].bitcast(I32), xs_picked[32 * q + 4 : 32 * q + 8, :].bitcast(I32)
+            )
+        xs_planes = [xs_picked, xs_moved]
+
+        gather_words(0, 0)
+        deal_scales(0)
+        gather_words(0, 1)
+        gather_words(1, 0)
+        gather_words(1, 1)
+        deal_words(1)
+        deal_scales(1)
+
+        down_raw = sbuf("down_raw", [P, 6 * N], U8, tag="xw_table0")
+        nc.sync.dma_start(down_raw[:, 0 : 4 * N].bitcast(I32), da_words[0].rearrange("p n t -> p (n t)").bitcast(I32))
+        nc.sync.dma_start(down_raw[:, 4 * N : 6 * N].bitcast(I32), db_words[0].bitcast(I32))
+        down_scales = reused("down_scales", [P, 2, N], U8, 8192)
+        nc.gpsimd.memset(down_scales[:].rearrange("p w n -> p (w n)").bitcast(I32), 0)
+        for w, scales in enumerate((da_scales, db_scales)):
+            for q in range(QUADS):
+                nc.sync.dma_start(
+                    down_scales[32 * q : 32 * q + 4, w, :].bitcast(I32), scales[0, 4 * q : 4 * q + 4, :].bitcast(I32)
+                )
+        for b in range(2):
+            pages[1, b] = reused("page1_%d" % b, [P, J], F32, 10240 + 4096 * b)
+            nc.gpsimd.memset(pages[1, b][:], 0.0)
+        ident = reused("ident", [P, P], F32, 9216)
+        make_identity(nc, ident[:])
+
+        hid = []
+        for t in range(PACK):
+            hid.append(sbuf("hid%d" % t, [P, J], F32))
+            for h in range(HALVES):
+                acc = bank("acc%d_%d" % (t, h), HALVES * t + h)
+                for z in range(PASSES):
+                    nc.tensor.matmul_mx(
+                        out=acc[:],
+                        lhsT=wa_dealt[t // 2][:, z, t % 2, :].bitcast(FP4X4),
+                        lhsT_scale=was_dealt[t // 2][:, z, t % 2, :],
+                        rhs=xw[z, h][:].bitcast(FP8X4),
+                        rhs_scale=xs_planes[z][:, h * BANK : (h + 1) * BANK],
+                        start=(z == 0),
+                        stop=(z == PASSES - 1),
+                    )
+                nc.scalar.activation(hid[t][:, h * BANK : (h + 1) * BANK], acc[:], RELU)
+
+        picked0 = sbuf("picked0", [P, PACK * I], BF16)
+        shared = reused("shared", [P, PACK * 2 * S], BF16, 20480)
+        woven1 = sbuf("woven1", [P, PACK * S], BF16)
+        picked = [
+            picked0[:].rearrange("p (t c) -> p t c", t=PACK),
+            shared[:].rearrange("p (t c) -> p t c", t=PACK)[:, :, 0:S],
+        ]
+        codes = [sbuf("codes%d" % w, [P, I], U32) for w in range(2)]
+        scales = [sbuf("scales%d" % w, [P, I], U8) for w in range(2)]
+
+        def pick(w, t):
+            nc.vector.tensor_copy(picked[w][:, t, :], hid[t][:].indirect(way_lists[w][:]))
+
+        def weave(w, dst, c0, c1):
+            nc.scalar.copy(
+                dst.rearrange("p (c t) -> p c t", t=PACK),
+                picked[w][:, :, c0:c1].rearrange("p t c -> p c t"),
+            )
+
+        def quantise(w, src, c0, c1):
+            nc.vector.quantize_mx(out=codes[w][:, c0:c1].bitcast(FP8X4), scales=scales[w][:, c0:c1], in_=src)
+
+        down_words = [
+            lambda m: down_raw[:, 4 * m * P : 4 * (m + 1) * P].bitcast(FP8X4),
+            lambda m: down_raw[:, 4 * N + 2 * m * P : 4 * N + 2 * (m + 1) * P].bitcast(FP4X4),
+        ]
+        prods = {}
+
+        def down(w, m):
+            acc = bank("down%d_%d" % (w, m), m)
+            nc.tensor.matmul_mx(
+                out=acc[:],
+                lhsT=down_words[w](m),
+                lhsT_scale=down_scales[:, w, m * P : (m + 1) * P],
+                rhs=codes[w][:].bitcast(FP8X4),
+                rhs_scale=scales[w][:],
+                start=True,
+                stop=True,
+            )
+            if (w, m) == (0, 1):
+                prods[w, m] = reused("prod0_1", [P, I], F32, 20480)
+            else:
+                prods[w, m] = sbuf("prod%d_%d" % (w, m), [P, I], F32)
+            nc.scalar.copy(prods[w, m][:], acc[:])
+
+        def place(w, m):
+            nc.vector.tensor_copy(pages[w, m % 2][:].indirect(way_lists[w][:]), prods[w, m][:])
+
+        def add_on_tensor(m):
+            for h in range(HALVES):
+                turned = bank("turned%d_%d" % (m, h), 4 + h)
+                for w in (1, 0):
+                    for b in range(BANK // P):
+                        nc.tensor.matmul(
+                            turned[:, b * P : (b + 1) * P],
+                            pages[w, m % 2][:, h * BANK + b * P : h * BANK + (b + 1) * P],
+                            ident[:],
+                            start=(w == 1 and b == 0),
+                            stop=(w == 0 and b == BANK // P - 1),
+                            is_transpose=True,
+                        )
+                summed = sbuf("summed%d_%d" % (m, h), [P, BANK], F32)
+                nc.scalar.copy(summed[:], turned[:])
+                back = bank("back%d_%d" % (m, h), 6 + h)
+                for b in range(BANK // P):
+                    nc.tensor.transpose(back[:, b * P : (b + 1) * P], summed[:, b * P : (b + 1) * P], ident[:])
+                result = sbuf("result%d_%d" % (m, h), [P, BANK], F32)
+                nc.scalar.copy(result[:], back[:])
+                nc.sync.dma_start(out[m * P : (m + 1) * P, h * BANK : (h + 1) * BANK], result[:])
+
+        def add_on_vector(m):
+            width = J // 4
+            for c in range(0, J, width):
+                result = sbuf("last%d" % c, [P, width], F32)
+                nc.vector.tensor_tensor(
+                    result[:], pages[0, m % 2][:, c : c + width], pages[1, m % 2][:, c : c + width], ADD
+                )
+                nc.sync.dma_start(out[m * P : (m + 1) * P, c : c + width], result[:])
+
+        for t in range(PACK):
+            pick(0, t)
+        woven0 = [shared[:, 4 * S : 6 * S], shared[:, S // 2 : S // 2 + 2 * S]]
+        for h in range(2):
+            weave(0, woven0[h], h * I // 2, (h + 1) * I // 2)
+        pick(1, 3)
+        quantise(0, woven0[0], 0, I // 2)
+        pick(1, 2)
+        quantise(0, woven0[1], I // 2, I)
+        pick(1, 1)
+        pick(1, 0)
+        down(0, 0)
+        weave(1, woven1[:], 0, S)
+        place(0, 0)
+        quantise(1, woven1[:], 0, S)
+        down(0, 1)
+        place(0, 1)
+        down(1, 0)
+        down(1, 1)
+        for m in range(2, TILES):
+            down(0, m)
+            down(1, m)
+        place(1, 0)
+        add_on_tensor(0)
+        place(1, 1)
+        add_on_tensor(1)
+        place(0, 2)
+        place(1, 2)
+        add_on_tensor(2)
+        place(0, 3)
+        place(1, 3)
+        add_on_vector(3)

@@ -50,24 +50,23 @@ def tile_list_expert_down_two_roads_kernel(
         way_lists = [lists.tile([P, I // LIST_ROWS], U16, name="way_list%d" % w) for w in range(2)]
 
         xs_table = sbuf("xs_table", [P, T], U8)
-        was_raw = reused("was_raw", [P, PASSES, R], U8, 13824)
+        was_raw = reused("was_raw", [P, PASSES, R], U8, 17408)
         xs_moved = sbuf("xs_moved", [P, J], U8)
         nc.vector.memset(xs_table[:, 0 : T // 2].bitcast(I32), 0)
         nc.gpsimd.memset(xs_table[:, T // 2 : T].bitcast(I32), 0)
         nc.vector.memset(was_raw[:].rearrange("p z n -> p (z n)").bitcast(I32), 0)
         nc.vector.memset(xs_moved[:].bitcast(I32), 0)
-        pages = {}
-        for b in range(2):
-            pages[0, b] = sbuf("page0_%d" % b, [P, J], F32)
-            nc.vector.memset(pages[0, b][:], 0.0)
+        pages = {(0, 0): sbuf("page0_0", [P, J], F32)}
+        nc.vector.memset(pages[0, 0][:], 0.0)
 
-        wa_raw = reused("wa_raw", [P, PASSES, 2 * R], U8, 8192)
+        wa_raw = reused("wa_raw", [P, PASSES, 2 * R], U8, 11776)
         nc.sync.dma_start(tok_list[:], offs)
         nc.scalar.dma_start(wa_raw[:].bitcast(I32), wa_words.rearrange("z p b -> p z b").bitcast(I32))
-        for q in range(QUADS):
-            queue = nc.sync if q < QUADS // 2 else nc.scalar
+        for r in range(4):
+            queue = nc.sync if r < 2 else nc.scalar
             queue.dma_start(
-                xs_table[32 * q : 32 * q + 8, :].bitcast(I32), xq_scales[:, 4 * q : 4 * q + 4, :].bitcast(I32)
+                xs_table[r:P:16, :].bitcast(I32),
+                xq_scales.rearrange("z (q r) n -> r q z n", r=4)[r].bitcast(I32),
             )
         xw_table = [sbuf("xw_table0", [P, T], I32), reused("xw_table1", [P, T], I32, 0)]
         for z in range(PASSES):
@@ -106,7 +105,7 @@ def tile_list_expert_down_two_roads_kernel(
         nc.vector.tensor_copy(xs_picked[:], xs_table[:].indirect(tok_list[:]))
         for q in range(QUADS):
             nc.scalar.dma_start(
-                xs_moved[32 * q : 32 * q + 4, :].bitcast(I32), xs_picked[32 * q + 4 : 32 * q + 8, :].bitcast(I32)
+                xs_moved[32 * q : 32 * q + 4, :].bitcast(I32), xs_picked[32 * q + 16 : 32 * q + 20, :].bitcast(I32)
             )
         xs_planes = [xs_picked, xs_moved]
 
@@ -121,17 +120,17 @@ def tile_list_expert_down_two_roads_kernel(
         down_raw = sbuf("down_raw", [P, 6 * N], U8, tag="xw_table0")
         nc.sync.dma_start(down_raw[:, 0 : 4 * N].bitcast(I32), da_words[0].rearrange("p n t -> p (n t)").bitcast(I32))
         nc.sync.dma_start(down_raw[:, 4 * N : 6 * N].bitcast(I32), db_words[0].bitcast(I32))
-        down_scales = reused("down_scales", [P, 2, N], U8, 8192)
+        down_scales = reused("down_scales", [P, 2, N], U8, 12288)
         nc.gpsimd.memset(down_scales[:].rearrange("p w n -> p (w n)").bitcast(I32), 0)
         for w, scales in enumerate((da_scales, db_scales)):
             for q in range(QUADS):
                 nc.sync.dma_start(
                     down_scales[32 * q : 32 * q + 4, w, :].bitcast(I32), scales[0, 4 * q : 4 * q + 4, :].bitcast(I32)
                 )
-        for b in range(2):
-            pages[1, b] = reused("page1_%d" % b, [P, J], F32, 10240 + 4096 * b)
-            nc.gpsimd.memset(pages[1, b][:], 0.0)
-        ident = reused("ident", [P, P], F32, 9216)
+        for w, b, offset in ((0, 1, 8192), (1, 0, 13824), (1, 1, 17920)):
+            pages[w, b] = reused("page%d_%d" % (w, b), [P, J], F32, offset)
+            nc.gpsimd.memset(pages[w, b][:], 0.0)
+        ident = reused("ident", [P, P], F32, 13312)
         make_identity(nc, ident[:])
 
         hid = []
@@ -152,7 +151,7 @@ def tile_list_expert_down_two_roads_kernel(
                 nc.scalar.activation(hid[t][:, h * BANK : (h + 1) * BANK], acc[:], RELU)
 
         picked0 = sbuf("picked0", [P, PACK * I], BF16)
-        shared = reused("shared", [P, PACK * 2 * S], BF16, 20480)
+        shared = reused("shared", [P, PACK * 2 * S], BF16, 22528)
         woven1 = sbuf("woven1", [P, PACK * S], BF16)
         picked = [
             picked0[:].rearrange("p (t c) -> p t c", t=PACK),
@@ -191,7 +190,7 @@ def tile_list_expert_down_two_roads_kernel(
                 stop=True,
             )
             if (w, m) == (0, 1):
-                prods[w, m] = reused("prod0_1", [P, I], F32, 20480)
+                prods[w, m] = reused("prod0_1", [P, I], F32, 22528)
             else:
                 prods[w, m] = sbuf("prod%d_%d" % (w, m), [P, I], F32)
             nc.scalar.copy(prods[w, m][:], acc[:])
@@ -202,14 +201,14 @@ def tile_list_expert_down_two_roads_kernel(
         def add_on_tensor(m):
             for h in range(HALVES):
                 turned = bank("turned%d_%d" % (m, h), 4 + h)
-                for w in (1, 0):
+                for w in range(2):
                     for b in range(BANK // P):
                         nc.tensor.matmul(
                             turned[:, b * P : (b + 1) * P],
                             pages[w, m % 2][:, h * BANK + b * P : h * BANK + (b + 1) * P],
                             ident[:],
-                            start=(w == 1 and b == 0),
-                            stop=(w == 0 and b == BANK // P - 1),
+                            start=(w == 0 and b == 0),
+                            stop=(w == 1 and b == BANK // P - 1),
                             is_transpose=True,
                         )
                 summed = sbuf("summed%d_%d" % (m, h), [P, BANK], F32)

@@ -68,20 +68,18 @@ def tile_list_expert_down_two_roads_kernel(
                 xs_table[r:P:16, :].bitcast(I32),
                 xq_scales.rearrange("z (q r) n -> r q z n", r=4)[r].bitcast(I32),
             )
-        xw_table = [sbuf("xw_table0", [P, T], I32), reused("xw_table1", [P, T], I32, 0)]
+        xw_table = [reused("xw_table0", [P, T], I32, 30720), reused("xw_table1", [P, T], I32, 0)]
         for z in range(PASSES):
             nc.sync.dma_start(xw_table[z][:], xq_words[z].rearrange("p n t -> p (n t)").bitcast(I32))
+            nc.sync.dma_start(way_lists[z][:], (offs2, offs3)[z])
         for q in range(QUADS):
-            queue = nc.scalar if q < QUADS // 2 else nc.gpsimd
-            queue.dma_start(
+            nc.scalar.dma_start(
                 was_raw[32 * q : 32 * q + 4, :, :].bitcast(I32),
                 wa_scales[:, 4 * q : 4 * q + 4, :].rearrange("z r n -> r z n").bitcast(I32),
             )
-        nc.sync.dma_start(way_lists[0][:], offs2)
-        nc.sync.dma_start(way_lists[1][:], offs3)
 
         wa_dealt = [sbuf("wa_dealt0", [P, PASSES, 2, 2 * P], U8), reused("wa_dealt1", [P, PASSES, 2, 2 * P], U8, 0)]
-        was_dealt = [sbuf("was_dealt0", [P, PASSES, 2, P], U8), reused("was_dealt1", [P, PASSES, 2, P], U8, 1024)]
+        was_dealt = [reused("was_dealt0", [P, PASSES, 2, P], U8, 30720), reused("was_dealt1", [P, PASSES, 2, P], U8, 1024)]
 
         def deal_words(g):
             by_slot = wa_raw[:].bitcast(U16).rearrange("p z (m t) -> p z t m", t=PACK)
@@ -110,14 +108,14 @@ def tile_list_expert_down_two_roads_kernel(
         xs_planes = [xs_picked, xs_moved]
 
         gather_words(0, 0)
-        deal_scales(0)
         gather_words(0, 1)
+        deal_scales(0)
         gather_words(1, 0)
         gather_words(1, 1)
         deal_words(1)
         deal_scales(1)
 
-        down_raw = sbuf("down_raw", [P, 6 * N], U8, tag="xw_table0")
+        down_raw = reused("down_raw", [P, 6 * N], U8, 31744)
         nc.sync.dma_start(down_raw[:, 0 : 4 * N].bitcast(I32), da_words[0].rearrange("p n t -> p (n t)").bitcast(I32))
         nc.sync.dma_start(down_raw[:, 4 * N : 6 * N].bitcast(I32), db_words[0].bitcast(I32))
         down_scales = reused("down_scales", [P, 2, N], U8, 12288)
@@ -165,8 +163,8 @@ def tile_list_expert_down_two_roads_kernel(
 
         def weave(w, dst, c0, c1):
             nc.scalar.copy(
-                dst.rearrange("p (c t) -> p c t", t=PACK),
-                picked[w][:, :, c0:c1].rearrange("p t c -> p c t"),
+                dst.rearrange("p (c i t) -> p c t i", i=4, t=PACK),
+                picked[w][:, :, c0:c1].rearrange("p t (c i) -> p c t i", i=4),
             )
 
         def quantise(w, src, c0, c1):

from contextlib import ExitStack

import concourse.mybir as mybir
from concourse.masks import make_identity

K, T, J, I, S, R, N = 1024, 2048, 1024, 512, 512, 512, 512
FLOPS = 2 * (K * R * J + R * N * I + R * N * S)

F32 = mybir.dt.float32
BF16 = mybir.dt.bfloat16
I32 = mybir.dt.int32
U32 = mybir.dt.uint32
U16 = mybir.dt.uint16
U8 = mybir.dt.uint8
FP8X4 = mybir.dt.float8_e4m3fn_x4
FP4X4 = mybir.dt.float4_e2m1fn_x4
RELU = mybir.ActivationFunctionType.Relu
ADD = mybir.AluOpType.add

P = 128
PACK = 4
PASSES = K // (P * PACK)
BANK = 512
HALVES = J // BANK
TILES = N // P
QUADS = 4
LIST_ROWS = 16


def tile_list_expert_down_two_roads_kernel(
    tc, xq_words, xq_scales, wa_words, wa_scales, da_words, da_scales, db_words, db_scales, offs, offs2, offs3, out
):
    nc = tc.nc
    with ExitStack() as ctx:
        lists = ctx.enter_context(tc.tile_pool(name="lists", bufs=1))
        sb = ctx.enter_context(tc.tile_pool(name="sb", bufs=1))
        late = ctx.enter_context(tc.tile_pool(name="late", bufs=1))
        psum = ctx.enter_context(tc.psum_pool(name="psum", bufs=1))

        def sbuf(name, shape, dtype, tag=None):
            return sb.tile(shape, dtype, name=name, tag=tag or name, align_bytes=64)

        def reused(name, shape, dtype, offset):
            return late.tile(shape, dtype, name=name, offset=offset, align_bytes=64)

        def bank(name, number):
            return psum.tile([P, BANK], F32, name=name, tag="bank%d" % number)

        tok_list = lists.tile([P, J // LIST_ROWS], U16, name="tok_list")
        way_lists = [lists.tile([P, I // LIST_ROWS], U16, name="way_list%d" % w) for w in range(2)]

        xs_table = sbuf("xs_table", [P, T], U8)
        was_raw = reused("was_raw", [P, PASSES, R], U8, 17408)
        xs_moved = sbuf("xs_moved", [P, J], U8)
        nc.vector.memset(xs_table[:, 0 : T // 2].bitcast(I32), 0)
        nc.gpsimd.memset(xs_table[:, T // 2 : T].bitcast(I32), 0)
        nc.vector.memset(was_raw[:].rearrange("p z n -> p (z n)").bitcast(I32), 0)
        nc.vector.memset(xs_moved[:].bitcast(I32), 0)
        pages = {(0, 0): sbuf("page0_0", [P, J], F32)}
        nc.vector.memset(pages[0, 0][:], 0.0)

        wa_raw = reused("wa_raw", [P, PASSES, 2 * R], U8, 11776)
        nc.sync.dma_start(tok_list[:], offs)
        nc.scalar.dma_start(wa_raw[:].bitcast(I32), wa_words.rearrange("z p b -> p z b").bitcast(I32))
        for r in range(4):
            queue = nc.sync if r < 2 else nc.scalar
            queue.dma_start(
                xs_table[r:P:16, :].bitcast(I32),
                xq_scales.rearrange("z (q r) n -> r q z n", r=4)[r].bitcast(I32),
            )
        xw_table = [reused("xw_table0", [P, T], I32, 30720), reused("xw_table1", [P, T], I32, 0)]
        for z in range(PASSES):
            nc.sync.dma_start(xw_table[z][:], xq_words[z].rearrange("p n t -> p (n t)").bitcast(I32))
            nc.sync.dma_start(way_lists[z][:], (offs2, offs3)[z])
        for q in range(QUADS):
            nc.scalar.dma_start(
                was_raw[32 * q : 32 * q + 4, :, :].bitcast(I32),
                wa_scales[:, 4 * q : 4 * q + 4, :].rearrange("z r n -> r z n").bitcast(I32),
            )

        wa_dealt = [sbuf("wa_dealt0", [P, PASSES, 2, 2 * P], U8), reused("wa_dealt1", [P, PASSES, 2, 2 * P], U8, 0)]
        was_dealt = [reused("was_dealt0", [P, PASSES, 2, P], U8, 30720), reused("was_dealt1", [P, PASSES, 2, P], U8, 1024)]

        def deal_words(g):
            by_slot = wa_raw[:].bitcast(U16).rearrange("p z (m t) -> p z t m", t=PACK)
            nc.vector.tensor_copy(wa_dealt[g][:].bitcast(U16), by_slot[:, :, 2 * g : 2 * g + 2, :])

        def deal_scales(g):
            by_slot = was_raw[:].rearrange("p z (m t) -> p z t m", t=PACK)
            nc.vector.tensor_copy(was_dealt[g][:], by_slot[:, :, 2 * g : 2 * g + 2, :])

        xw = {}

        def gather_words(z, h):
            xw[z, h] = sbuf("xw%d_%d" % (z, h), [P, BANK], U32)
            cols = BANK // LIST_ROWS
            nc.vector.tensor_copy(
                xw[z, h][:], xw_table[z][:].bitcast(U32).indirect(tok_list[:, h * cols : (h + 1) * cols])
            )

        deal_words(0)
        xs_picked = sbuf("xs_picked", [P, J], U8)
        nc.vector.tensor_copy(xs_picked[:], xs_table[:].indirect(tok_list[:]))
        for q in range(QUADS):
            nc.scalar.dma_start(
                xs_moved[32 * q : 32 * q + 4, :].bitcast(I32), xs_picked[32 * q + 16 : 32 * q + 20, :].bitcast(I32)
            )
        xs_planes = [xs_picked, xs_moved]

        gather_words(0, 0)
        gather_words(0, 1)
        deal_scales(0)
        gather_words(1, 0)
        gather_words(1, 1)
        deal_words(1)
        deal_scales(1)

        down_raw = reused("down_raw", [P, 6 * N], U8, 31744)
        nc.sync.dma_start(down_raw[:, 0 : 4 * N].bitcast(I32), da_words[0].rearrange("p n t -> p (n t)").bitcast(I32))
        nc.sync.dma_start(down_raw[:, 4 * N : 6 * N].bitcast(I32), db_words[0].bitcast(I32))
        down_scales = reused("down_scales", [P, 2, N], U8, 12288)
        nc.gpsimd.memset(down_scales[:].rearrange("p w n -> p (w n)").bitcast(I32), 0)
        for w, scales in enumerate((da_scales, db_scales)):
            for q in range(QUADS):
                nc.sync.dma_start(
                    down_scales[32 * q : 32 * q + 4, w, :].bitcast(I32), scales[0, 4 * q : 4 * q + 4, :].bitcast(I32)
                )
        for w, b, offset in ((0, 1, 8192), (1, 0, 13824), (1, 1, 17920)):
            pages[w, b] = reused("page%d_%d" % (w, b), [P, J], F32, offset)
            nc.gpsimd.memset(pages[w, b][:], 0.0)
        ident = reused("ident", [P, P], F32, 13312)
        make_identity(nc, ident[:])

        hid = []
        for t in range(PACK):
            hid.append(sbuf("hid%d" % t, [P, J], F32))
            for h in range(HALVES):
                acc = bank("acc%d_%d" % (t, h), HALVES * t + h)
                for z in range(PASSES):
                    nc.tensor.matmul_mx(
                        out=acc[:],
                        lhsT=wa_dealt[t // 2][:, z, t % 2, :].bitcast(FP4X4),
                        lhsT_scale=was_dealt[t // 2][:, z, t % 2, :],
                        rhs=xw[z, h][:].bitcast(FP8X4),
                        rhs_scale=xs_planes[z][:, h * BANK : (h + 1) * BANK],
                        start=(z == 0),
                        stop=(z == PASSES - 1),
                    )
                nc.scalar.activation(hid[t][:, h * BANK : (h + 1) * BANK], acc[:], RELU)

        picked0 = sbuf("picked0", [P, PACK * I], BF16)
        shared = reused("shared", [P, PACK * 2 * S], BF16, 22528)
        woven1 = sbuf("woven1", [P, PACK * S], BF16)
        picked = [
            picked0[:].rearrange("p (t c) -> p t c", t=PACK),
            shared[:].rearrange("p (t c) -> p t c", t=PACK)[:, :, 0:S],
        ]
        codes = [sbuf("codes%d" % w, [P, I], U32) for w in range(2)]
        scales = [sbuf("scales%d" % w, [P, I], U8) for w in range(2)]

        def pick(w, t):
            nc.vector.tensor_copy(picked[w][:, t, :], hid[t][:].indirect(way_lists[w][:]))

        def weave(w, dst, c0, c1):
            nc.scalar.copy(
                dst.rearrange("p (c i t) -> p c t i", i=4, t=PACK),
                picked[w][:, :, c0:c1].rearrange("p t (c i) -> p c t i", i=4),
            )

        def quantise(w, src, c0, c1):
            nc.vector.quantize_mx(out=codes[w][:, c0:c1].bitcast(FP8X4), scales=scales[w][:, c0:c1], in_=src)

        down_words = [
            lambda m: down_raw[:, 4 * m * P : 4 * (m + 1) * P].bitcast(FP8X4),
            lambda m: down_raw[:, 4 * N + 2 * m * P : 4 * N + 2 * (m + 1) * P].bitcast(FP4X4),
        ]
        prods = {}

        def down(w, m):
            acc = bank("down%d_%d" % (w, m), m)
            nc.tensor.matmul_mx(
                out=acc[:],
                lhsT=down_words[w](m),
                lhsT_scale=down_scales[:, w, m * P : (m + 1) * P],
                rhs=codes[w][:].bitcast(FP8X4),
                rhs_scale=scales[w][:],
                start=True,
                stop=True,
            )
            if (w, m) == (0, 1):
                prods[w, m] = reused("prod0_1", [P, I], F32, 22528)
            else:
                prods[w, m] = sbuf("prod%d_%d" % (w, m), [P, I], F32)
            nc.scalar.copy(prods[w, m][:], acc[:])

        def place(w, m):
            nc.vector.tensor_copy(pages[w, m % 2][:].indirect(way_lists[w][:]), prods[w, m][:])

        def add_on_tensor(m):
            for h in range(HALVES):
                turned = bank("turned%d_%d" % (m, h), 4 + h)
                for w in range(2):
                    for b in range(BANK // P):
                        nc.tensor.matmul(
                            turned[:, b * P : (b + 1) * P],
                            pages[w, m % 2][:, h * BANK + b * P : h * BANK + (b + 1) * P],
                            ident[:],
                            start=(w == 0 and b == 0),
                            stop=(w == 1 and b == BANK // P - 1),
                            is_transpose=True,
                        )
                summed = sbuf("summed%d_%d" % (m, h), [P, BANK], F32)
                nc.scalar.copy(summed[:], turned[:])
                back = bank("back%d_%d" % (m, h), 6 + h)
                for b in range(BANK // P):
                    nc.tensor.transpose(back[:, b * P : (b + 1) * P], summed[:, b * P : (b + 1) * P], ident[:])
                result = sbuf("result%d_%d" % (m, h), [P, BANK], F32)
                nc.scalar.copy(result[:], back[:])
                nc.sync.dma_start(out[m * P : (m + 1) * P, h * BANK : (h + 1) * BANK], result[:])

        def add_on_vector(m):
            width = J // 4
            for c in range(0, J, width):
                result = sbuf("last%d" % c, [P, width], F32)
                nc.vector.tensor_tensor(
                    result[:], pages[0, m % 2][:, c : c + width], pages[1, m % 2][:, c : c + width], ADD
                )
                nc.sync.dma_start(out[m * P : (m + 1) * P, c : c + width], result[:])

        for t in range(PACK):
            pick(0, t)
        woven0 = [shared[:, 4 * S : 6 * S], shared[:, S // 2 : S // 2 + 2 * S]]
        for h in range(2):
            weave(0, woven0[h], h * I // 2, (h + 1) * I // 2)
        pick(1, 3)
        quantise(0, woven0[0], 0, I // 2)
        pick(1, 2)
        quantise(0, woven0[1], I // 2, I)
        pick(1, 1)
        pick(1, 0)
        down(0, 0)
        weave(1, woven1[:], 0, S)
        place(0, 0)
        quantise(1, woven1[:], 0, S)
        down(0, 1)
        place(0, 1)
        down(1, 0)
        down(1, 1)
        for m in range(2, TILES):
            down(0, m)
            down(1, m)
        place(1, 0)
        add_on_tensor(0)
        place(1, 1)
        add_on_tensor(1)
        place(0, 2)
        place(1, 2)
        add_on_tensor(2)
        place(0, 3)
        place(1, 3)
        add_on_vector(3)
